import numpy as np
import ml_dtypes


def mxq(x, axis, fmt="e4m3"):
    dtype, down = {"e4m3": (ml_dtypes.float8_e4m3fn, 7), "e5m2": (ml_dtypes.float8_e5m2, 14)}[fmt]
    v = np.moveaxis(np.asarray(x, np.float32).astype(ml_dtypes.bfloat16).astype(np.float64), axis, -1)
    blocks = v.reshape(v.shape[:-1] + (-1, 32))
    amax = np.abs(blocks).max(-1, keepdims=True)
    byte = np.maximum(np.where(amax > 0, np.frexp(amax)[1] - 1 + 127, 0) - down, 1)
    scale = np.exp2(byte - 127.0)
    codes = (blocks / scale).astype(np.float32).astype(dtype).astype(np.float64)
    return np.moveaxis((codes * scale).reshape(v.shape), -1, axis)


WIDE = False


def mx_kscale(k):
    if not WIDE:
        return np.ones(k)
    levels = np.array([10, -10, 5, -5, 0])
    if k % 512:
        return np.exp2(np.random.permutation(np.resize(levels, k // 32))).repeat(32)
    a = np.empty((k // 512, 16))
    for p in range(k // 512):
        a[p, :8] = np.random.permutation(np.resize(levels, 8))
        for g in range(8):
            far = levels[np.abs(levels - a[p, g]) >= 10]
            a[p, g + 8] = far[np.random.randint(len(far))]
    return np.exp2(a.ravel()).repeat(32)


def f64(x):
    return np.asarray(x).astype(np.float64)


def striped(idx):
    return np.tile(np.asarray(idx).reshape(-1, 16).T, (8, 1)).astype(np.uint16)


def unstriped(offs):
    return offs[:16].T.reshape(-1).astype(np.int64)


E2M1 = np.array([0.0, 0.5, 1.0, 1.5, 2.0, 3.0, 4.0, 6.0, -0.0, -0.5, -1.0, -1.5, -2.0, -3.0, -4.0, -6.0])


def pack_weight(w, fmt):
    k, n = w.shape
    w = f64(np.asarray(w, np.float32).astype(ml_dtypes.bfloat16)).reshape(k // 32, 32, n)
    amax = np.abs(w).max(1)
    if fmt == "e4m3":
        byte = np.frexp(amax)[1] - 1 + 127 - 7
    else:
        mant, ex = np.frexp(amax / 6.0)
        byte = np.where(mant > 0.5, ex, ex - 1) + 127
    byte = np.clip(np.where(amax > 0, byte, 1), 1, 254)
    scaled = (w * np.exp2(127.0 - byte)[:, None, :]).reshape(k, n).astype(np.float32)
    by_word = np.ascontiguousarray(scaled.reshape(k // 512, 128, 4, n).transpose(0, 1, 3, 2))
    if fmt == "e4m3":
        words = by_word.astype(ml_dtypes.float8_e4m3fn).view(np.uint8)
    else:
        c = by_word.astype(ml_dtypes.float4_e2m1fn).view(np.uint8) & 0xF
        words = (c[..., 0::2] | (c[..., 1::2] << 4)).reshape(k // 512, 128, 2 * n)
    return np.ascontiguousarray(words), np.ascontiguousarray(byte.astype(np.uint8).reshape(k // 512, 16, n))


def unpack_weight(words, scales, fmt):
    g, _, n = scales.shape
    words = np.ascontiguousarray(words).reshape(g, 128, n, -1)
    if fmt == "e4m3":
        vals = words.view(ml_dtypes.float8_e4m3fn).astype(np.float64)
    else:
        nib = np.empty((g, 128, n, 4), np.uint8)
        nib[..., 0::2] = words & 0xF
        nib[..., 1::2] = words >> 4
        vals = E2M1[nib]
    vals = vals * np.repeat(np.exp2(scales.astype(np.float64) - 127.0), 8, axis=1)[..., None]
    return vals.transpose(0, 1, 3, 2).reshape(g * 512, n)


def sigmoid(v):
    return 1.0 / (1.0 + np.exp(-v))


def bf(x):
    return np.asarray(x, np.float32).astype(ml_dtypes.bfloat16)


def planes(Y):
    r, m = Y.shape
    b = f64(bf(Y)).reshape(r // 32, 32, m)
    amax = np.abs(b).max(1)
    byte = np.clip(np.where(amax > 0, np.frexp(amax)[1] - 1 + 127 - 7, 1), 1, 254)
    codes = (b * np.exp2(127.0 - byte)[:, None, :]).reshape(r, m).astype(np.float32).astype(ml_dtypes.float8_e4m3fn).view(np.uint8)
    words = codes.reshape(r // 512, 128, 4, m).transpose(0, 1, 3, 2)
    return np.ascontiguousarray(words), np.ascontiguousarray(byte.astype(np.uint8).reshape(r // 512, 16, m))


D, T, I, Q, E = 512, 2048, 512, 256, 512


def setup_inputs():
    n = np.random.standard_normal
    idx = np.random.permutation(T)[:I]
    fd = mx_kscale(D)
    fi = mx_kscale(I)
    keysp = pack_weight(n((D, T)) / fd[:, None], "e2m1")
    return {
        "query": (n((D, Q)) * 1.0 / np.sqrt(D) * fd[:, None]).astype(np.float32),
        "keys_words": keysp[0],
        "keys_scales": keysp[1],
        "bias": (np.random.uniform(-1.0, 1.0, (I, 1))).astype(np.float32),
        "vals": (n((E, T)) * np.random.uniform(0.3, 2.0, (1, T))).astype(np.float32),
        "us": (np.random.uniform(0.02, 0.1, (I, 1)) * fi[:, None]).astype(np.float32),
        "vsc": (np.random.uniform(0.5, 2.0, (I, 1)) / fi[:, None]).astype(np.float32),
        "offs": striped(idx),
    }


def reference(query, keys_words, keys_scales, bias, vals, us, vsc, offs):
    idx = unstriped(offs)
    keysu = unpack_weight(keys_words, keys_scales, "e2m1")
    keysidxg = keysu[:, idx]
    queryq = mxq(f64(query), 0, "e4m3")
    a = keysidxg.T @ queryq
    vt = f64(vals)[:, idx].T
    w = sigmoid(a + f64(bias)) * np.sqrt(np.mean(np.square(vt), axis=1, keepdims=True)) * f64(us)
    vv = vt * f64(vsc)
    vvq = mxq(vv, 0, "e4m3")
    wq = mxq(w, 0, "e4m3")
    o = vvq.T @ wq
    words, scales = planes(o)
    return o, words, scales

@@ -1,0 +1,200 @@
+from contextlib import ExitStack
+
+import concourse.mybir as mybir
+from concourse.masks import make_identity
+
+D, T, I, Q, E = 512, 2048, 512, 256, 512
+FLOPS = 2 * D * I * Q + 2 * I * E * Q
+
+F32 = mybir.dt.float32
+BF16 = mybir.dt.bfloat16
+I32 = mybir.dt.int32
+U32 = mybir.dt.uint32
+U16 = mybir.dt.uint16
+U8 = mybir.dt.uint8
+FP8X4 = mybir.dt.float8_e4m3fn_x4
+FP4X4 = mybir.dt.float4_e2m1fn_x4
+ACT = mybir.ActivationFunctionType
+ALU = mybir.AluOpType
+
+P = 128
+PACK = 4
+HALVES = 2
+QH = Q // HALVES
+RUN = 4
+POOL_BYTES = T * 4
+SLOT_BYTES = I * 4
+
+
+def tile_attend_valuelength_pl_kernel(tc, query, keys_words, keys_scales, bias, vals, us, vsc, offs, out_0, out_1, out_2):
+    nc = tc.nc
+
+    with ExitStack() as ctx:
+        sb = ctx.enter_context(tc.tile_pool(name="sb", bufs=1))
+        ring = ctx.enter_context(tc.tile_pool(name="ring", bufs=1))
+        big = ctx.enter_context(tc.tile_pool(name="big", bufs=1))
+        ps = ctx.enter_context(tc.psum_pool(name="ps", bufs=1))
+
+        offsets = sb.tile([P, I // 16], U16, name="offsets")
+        nc.sync.dma_start(offsets[:], offs)
+
+        key_pool = sb.tile([P, T], U16, name="key_pool")
+        nc.sync.dma_start(key_pool[:].bitcast(I32), keys_words[0].bitcast(I32))
+
+        q_raw = sb.tile([P, PACK, Q], F32, name="q_raw")
+        nc.sync.dma_start(q_raw[:], query.rearrange("(p t) q -> p t q", t=PACK))
+
+        val_rows = vals.rearrange("(p j) n -> p j n", j=PACK)
+        val_pool = [big.tile([P, T], F32, name="val_pool%d" % j, align_bytes=64, offset=j * POOL_BYTES) for j in range(PACK)]
+        for j in range(PACK):
+            nc.sync.dma_start(val_pool[j][:], val_rows[:, j, :])
+
+        bias_t = sb.tile([P, PACK], F32, name="bias_t")
+        vsc_t = sb.tile([P, PACK], F32, name="vsc_t")
+        us_t = sb.tile([P, PACK], F32, name="us_t")
+        for dst, src in ((bias_t, bias), (vsc_t, vsc), (us_t, us)):
+            nc.scalar.dma_start(dst[:], src.rearrange("(p t) o -> p (t o)", t=PACK))
+
+        scale_pool = sb.tile([P, T], U8, name="scale_pool")
+        nc.gpsimd.memset(scale_pool[:].bitcast(I32), 0)
+        for quad in range(4):
+            nc.scalar.dma_start(
+                scale_pool[32 * quad : 32 * quad + 4, :].bitcast(I32),
+                keys_scales[0, 4 * quad : 4 * quad + 4, :].bitcast(I32),
+            )
+
+        ident = sb.tile([P, P], F32, name="ident")
+        make_identity(nc, ident[:])
+
+        key_listed = sb.tile([P, I], U16, name="key_listed")
+        nc.vector.tensor_copy(key_listed[:], key_pool[:].indirect(offsets[:]))
+        key_dealt = sb.tile([P, PACK, P], U16, name="key_dealt", align_bytes=64)
+        nc.vector.tensor_copy(key_dealt[:], key_listed[:].rearrange("p (s t) -> p t s", t=PACK))
+        scale_dealt = sb.tile([P, PACK, P], U8, name="scale_dealt", align_bytes=64)
+        nc.vector.tensor_copy(scale_dealt[:].rearrange("p t s -> p s t"), scale_pool[:].indirect(offsets[:]))
+
+        q_bf = ring.tile([P, Q, PACK], BF16, name="q_bf", align_bytes=64, offset=SLOT_BYTES // 2)
+        nc.scalar.copy(
+            q_bf[:].rearrange("p (c i) t -> p c t i", i=RUN),
+            q_raw[:].rearrange("p t (c i) -> p c t i", i=RUN),
+        )
+        q_codes = sb.tile([P, Q], U32, name="q_codes", align_bytes=64)
+        q_scales = sb.tile([P, Q], U8, name="q_scales", align_bytes=64)
+        nc.vector.quantize_mx(q_codes[:].bitcast(FP8X4), q_scales[:], q_bf[:].rearrange("p q t -> p (q t)"))
+
+        scores = [ps.tile([P, 2, Q], F32, name="scores%d" % b, tag="products", bufs=2) for b in range(2)]
+        for t in range(PACK):
+            nc.tensor.matmul_mx(
+                scores[t // 2][:, t % 2, :],
+                lhsT=key_dealt[:, t, :].bitcast(FP4X4),
+                lhsT_scale=scale_dealt[:, t, :],
+                rhs=q_codes[:].bitcast(FP8X4),
+                rhs_scale=q_scales[:],
+                start=True,
+                stop=True,
+            )
+        gate = sb.tile([P, PACK, Q], F32, name="gate")
+        gate_us = sb.tile([P, PACK, Q], F32, name="gate_us")
+        for t in range(PACK):
+            nc.scalar.activation(gate[:, t, :], scores[t // 2][:, t % 2, :], ACT.Sigmoid, bias=bias_t[:, t : t + 1])
+        for t in range(PACK):
+            nc.scalar.activation(gate_us[:, t, :], gate[:, t, :], ACT.Copy, scale=us_t[:, t : t + 1])
+
+        vv_codes = sb.tile([P, PACK, P], U32, name="vv_codes", align_bytes=64)
+        vv_scales = sb.tile([P, PACK, P], U8, name="vv_scales", align_bytes=64)
+        mean_sq = []
+        turned = []
+
+        def gather_and_turn(j):
+            listed = ring.tile([P, PACK, P], F32, name="val_listed%d" % j, align_bytes=64, offset=(j % 2) * SLOT_BYTES)
+            nc.vector.tensor_copy(listed[:].rearrange("p t s -> p s t"), val_pool[j][:].indirect(offsets[:]))
+            squares = sb.tile([P, PACK, P], BF16, name="squares%d" % j)
+            part = sb.tile([P, PACK], F32, name="mean_sq%d" % j)
+            for t in range(PACK):
+                for_squares = ps.tile([P, P], F32, name="for_squares", tag="for_squares", bufs=PACK)
+                nc.tensor.transpose(for_squares[:], listed[:, t, :], ident[:])
+                nc.scalar.activation(
+                    squares[:, t, :], for_squares[:], ACT.Square, scale=E**-0.5, accum_out=part[:, t : t + 1]
+                )
+            for_values = ps.tile([P, PACK, P], F32, name="for_values", tag="for_values", bufs=2)
+            for t in range(PACK):
+                nc.tensor.transpose(for_values[:, t, :], listed[:, t, :], ident[:])
+            mean_sq.append(part)
+            turned.append(for_values)
+
+        def scale_and_quantise(j):
+            vv_bf = big.tile([P, P, PACK], BF16, name="vv_bf%d" % j, align_bytes=64, offset=(j + 1) % PACK * POOL_BYTES)
+            nc.vector.tensor_tensor(
+                vv_bf[:],
+                turned[j][:].rearrange("p t e -> p e t"),
+                vsc_t[:].unsqueeze(1).to_broadcast([P, P, PACK]),
+                ALU.mult,
+            )
+            nc.vector.quantize_mx(
+                vv_codes[:, j, :].bitcast(FP8X4), vv_scales[:, j, :], vv_bf[:].rearrange("p e t -> p (e t)")
+            )
+
+        for j in range(PACK + 1):
+            if j < PACK:
+                gather_and_turn(j)
+            if j > 0:
+                scale_and_quantise(j - 1)
+
+        early = mean_sq[0]
+        for j in range(1, PACK - 1):
+            more = sb.tile([P, PACK], F32, name="early%d" % j)
+            nc.gpsimd.tensor_tensor(more[:], early[:], mean_sq[j][:], ALU.add)
+            early = more
+        rms = sb.tile([P, PACK], F32, name="rms")
+        for t in range(PACK):
+            nc.scalar.activation(rms[:, t : t + 1], mean_sq[-1][:, t : t + 1], ACT.Sqrt, bias=early[:, t : t + 1])
+
+        out_rows = out_0.rearrange("(p j) q -> p j q", j=PACK)
+        out_words = out_1[0].rearrange("p c r -> p (c r)").bitcast(I32)
+        o_codes = sb.tile([P, Q], U32, name="o_codes", align_bytes=64)
+        o_scales = sb.tile([P, Q], U8, name="o_scales", align_bytes=64)
+        sums = []
+        for h in range(HALVES):
+            cols = slice(h * QH, (h + 1) * QH)
+            w_bf = sb.tile([P, QH, PACK], BF16, name="w_bf%d" % h, align_bytes=64)
+            nc.vector.tensor_tensor(
+                w_bf[:].rearrange("p (c i) t -> p c t i", i=RUN),
+                gate_us[:, :, cols].rearrange("p t (c i) -> p c t i", i=RUN),
+                rms[:].unsqueeze(1).unsqueeze(3).to_broadcast([P, QH // RUN, PACK, RUN]),
+                ALU.mult,
+            )
+            w_codes = sb.tile([P, QH], U32, name="w_codes%d" % h, align_bytes=64)
+            w_scales = sb.tile([P, QH], U8, name="w_scales%d" % h, align_bytes=64)
+            nc.vector.quantize_mx(w_codes[:].bitcast(FP8X4), w_scales[:], w_bf[:].rearrange("p q t -> p (q t)"))
+            bank = ps.tile([P, PACK, QH], F32, name="sums%d" % h, tag="products", bufs=2)
+            for j in range(PACK):
+                nc.tensor.matmul_mx(
+                    bank[:, j, :],
+                    lhsT=vv_codes[:, j, :].bitcast(FP8X4),
+                    lhsT_scale=vv_scales[:, j, :],
+                    rhs=w_codes[:].bitcast(FP8X4),
+                    rhs_scale=w_scales[:],
+                    start=True,
+                    stop=True,
+                )
+            sums.append(bank)
+
+        for h in range(HALVES):
+            cols = slice(h * QH, (h + 1) * QH)
+            o_bf = sb.tile([P, QH, PACK], BF16, name="o_bf%d" % h, align_bytes=64)
+            nc.scalar.copy(o_bf[:], sums[h][:].rearrange("p j q -> p q j"))
+            nc.vector.quantize_mx(o_codes[:, cols].bitcast(FP8X4), o_scales[:, cols], o_bf[:].rearrange("p q j -> p (q j)"))
+            nc.sync.dma_start(out_words[:, cols], o_codes[:, cols].bitcast(I32))
+            o_f32 = sb.tile([P, PACK, QH], F32, name="o_f32%d" % h)
+            if h < HALVES - 1:
+                nc.vector.tensor_copy(o_f32[:], sums[h][:])
+                nc.sync.dma_start(out_rows[:, :, cols], o_f32[:])
+            else:
+                nc.scalar.copy(o_f32[:], sums[h][:])
+                nc.scalar.dma_start(out_rows[:, :, cols], o_f32[:])
+        for quad in range(4):
+            queue = nc.sync if quad < 2 else nc.scalar
+            queue.dma_start(
+                out_2[0, 4 * quad : 4 * quad + 4, :].bitcast(I32),
+                o_scales[32 * quad : 32 * quad + 4, :].bitcast(I32),
+            )

@@ -22,6 +22,7 @@ PACK = 4
 HALVES = 2
 QH = Q // HALVES
 RUN = 4
+VV_BF_BYTES = P * PACK * 2
 POOL_BYTES = T * 4
 SLOT_BYTES = I * 4
 
@@ -41,27 +42,30 @@ def tile_attend_valuelength_pl_kernel(tc, query, keys_words, keys_scales, bias, 
         key_pool = sb.tile([P, T], U16, name="key_pool")
         nc.sync.dma_start(key_pool[:].bitcast(I32), keys_words[0].bitcast(I32))
 
-        q_raw = sb.tile([P, PACK, Q], F32, name="q_raw")
-        nc.sync.dma_start(q_raw[:], query.rearrange("(p t) q -> p t q", t=PACK))
-
-        val_rows = vals.rearrange("(p j) n -> p j n", j=PACK)
-        val_pool = [big.tile([P, T], F32, name="val_pool%d" % j, align_bytes=64, offset=j * POOL_BYTES) for j in range(PACK)]
-        for j in range(PACK):
-            nc.sync.dma_start(val_pool[j][:], val_rows[:, j, :])
-
-        bias_t = sb.tile([P, PACK], F32, name="bias_t")
-        vsc_t = sb.tile([P, PACK], F32, name="vsc_t")
-        us_t = sb.tile([P, PACK], F32, name="us_t")
-        for dst, src in ((bias_t, bias), (vsc_t, vsc), (us_t, us)):
-            nc.scalar.dma_start(dst[:], src.rearrange("(p t) o -> p (t o)", t=PACK))
-
         scale_pool = sb.tile([P, T], U8, name="scale_pool")
-        nc.gpsimd.memset(scale_pool[:].bitcast(I32), 0)
+        nc.vector.memset(scale_pool[:].bitcast(I32), 0)
         for quad in range(4):
-            nc.scalar.dma_start(
+            nc.sync.dma_start(
                 scale_pool[32 * quad : 32 * quad + 4, :].bitcast(I32),
                 keys_scales[0, 4 * quad : 4 * quad + 4, :].bitcast(I32),
             )
+
+        q_raw = sb.tile([P, PACK, Q], F32, name="q_raw")
+        nc.sync.dma_start(q_raw[:], query.rearrange("(p t) q -> p t q", t=PACK))
+
+        def load_by_slot(name, src):
+            dst = sb.tile([P, PACK], F32, name=name)
+            nc.sync.dma_start(dst[:], src.rearrange("(p t) o -> p (t o)", t=PACK))
+            return dst
+
+        val_rows = vals.rearrange("(p j) n -> p j n", j=PACK)
+        val_pool = [big.tile([P, T], F32, name="val_pool%d" % j, align_bytes=64, offset=j * POOL_BYTES) for j in range(PACK)]
+        bias_t = load_by_slot("bias_t", bias)
+        nc.sync.dma_start(val_pool[0][:], val_rows[:, 0, :])
+        vsc_t = load_by_slot("vsc_t", vsc)
+        us_t = load_by_slot("us_t", us)
+        for j in range(1, PACK):
+            nc.sync.dma_start(val_pool[j][:], val_rows[:, j, :])
 
         ident = sb.tile([P, P], F32, name="ident")
         make_identity(nc, ident[:])
@@ -71,7 +75,9 @@ def tile_attend_valuelength_pl_kernel(tc, query, keys_words, keys_scales, bias, 
         key_dealt = sb.tile([P, PACK, P], U16, name="key_dealt", align_bytes=64)
         nc.vector.tensor_copy(key_dealt[:], key_listed[:].rearrange("p (s t) -> p t s", t=PACK))
         scale_dealt = sb.tile([P, PACK, P], U8, name="scale_dealt", align_bytes=64)
-        nc.vector.tensor_copy(scale_dealt[:].rearrange("p t s -> p s t"), scale_pool[:].indirect(offsets[:]))
+        scale_listed = sb.tile([P, I], U8, name="scale_listed")
+        nc.vector.tensor_copy(scale_listed[:], scale_pool[:].indirect(offsets[:]))
+        nc.vector.tensor_copy(scale_dealt[:], scale_listed[:].rearrange("p (s t) -> p t s", t=PACK))
 
         q_bf = ring.tile([P, Q, PACK], BF16, name="q_bf", align_bytes=64, offset=SLOT_BYTES // 2)
         nc.scalar.copy(
@@ -94,35 +100,34 @@ def tile_attend_valuelength_pl_kernel(tc, query, keys_words, keys_scales, bias, 
                 stop=True,
             )
         gate = sb.tile([P, PACK, Q], F32, name="gate")
-        gate_us = sb.tile([P, PACK, Q], F32, name="gate_us")
         for t in range(PACK):
             nc.scalar.activation(gate[:, t, :], scores[t // 2][:, t % 2, :], ACT.Sigmoid, bias=bias_t[:, t : t + 1])
-        for t in range(PACK):
-            nc.scalar.activation(gate_us[:, t, :], gate[:, t, :], ACT.Copy, scale=us_t[:, t : t + 1])
 
-        vv_codes = sb.tile([P, PACK, P], U32, name="vv_codes", align_bytes=64)
-        vv_scales = sb.tile([P, PACK, P], U8, name="vv_scales", align_bytes=64)
+        root_table = sb.tile([P, 1], F32, name="root_table")
+        nc.scalar.activation(root_table[:], gate[:, PACK - 1, 0:1], ACT.Sqrt)
+
+        vv_mx = []
         mean_sq = []
         turned = []
 
         def gather_and_turn(j):
-            listed = ring.tile([P, PACK, P], F32, name="val_listed%d" % j, align_bytes=64, offset=(j % 2) * SLOT_BYTES)
-            nc.vector.tensor_copy(listed[:].rearrange("p t s -> p s t"), val_pool[j][:].indirect(offsets[:]))
+            listed = ring.tile([P, I], F32, name="val_listed%d" % j, align_bytes=64, offset=(j % 2) * SLOT_BYTES)
+            nc.vector.tensor_copy(listed[:], val_pool[j][:].indirect(offsets[:]))
             squares = sb.tile([P, PACK, P], BF16, name="squares%d" % j)
             part = sb.tile([P, PACK], F32, name="mean_sq%d" % j)
             for t in range(PACK):
                 for_squares = ps.tile([P, P], F32, name="for_squares", tag="for_squares", bufs=PACK)
-                nc.tensor.transpose(for_squares[:], listed[:, t, :], ident[:])
+                nc.tensor.transpose(for_squares[:], listed[:, t::PACK], ident[:])
                 nc.scalar.activation(
                     squares[:, t, :], for_squares[:], ACT.Square, scale=E**-0.5, accum_out=part[:, t : t + 1]
                 )
             for_values = ps.tile([P, PACK, P], F32, name="for_values", tag="for_values", bufs=2)
             for t in range(PACK):
-                nc.tensor.transpose(for_values[:, t, :], listed[:, t, :], ident[:])
+                nc.tensor.transpose(for_values[:, t, :], listed[:, t::PACK], ident[:])
             mean_sq.append(part)
             turned.append(for_values)
 
-        def scale_and_quantise(j):
+        def scale_values(j):
             vv_bf = big.tile([P, P, PACK], BF16, name="vv_bf%d" % j, align_bytes=64, offset=(j + 1) % PACK * POOL_BYTES)
             nc.vector.tensor_tensor(
                 vv_bf[:],
@@ -130,48 +135,74 @@ def tile_attend_valuelength_pl_kernel(tc, query, keys_words, keys_scales, bias, 
                 vsc_t[:].unsqueeze(1).to_broadcast([P, P, PACK]),
                 ALU.mult,
             )
-            nc.vector.quantize_mx(
-                vv_codes[:, j, :].bitcast(FP8X4), vv_scales[:, j, :], vv_bf[:].rearrange("p e t -> p (e t)")
-            )
+            return vv_bf
 
-        for j in range(PACK + 1):
-            if j < PACK:
-                gather_and_turn(j)
-            if j > 0:
-                scale_and_quantise(j - 1)
+        def quantise_values(j, vv_bf):
+            codes = big.tile(
+                [P, P], U32, name="vv_codes%d" % j, align_bytes=64, offset=(j + 2) % PACK * POOL_BYTES + VV_BF_BYTES
+            )
+            scales = sb.tile([P, P], U8, name="vv_scales%d" % j, align_bytes=64)
+            nc.vector.quantize_mx(codes[:].bitcast(FP8X4), scales[:], vv_bf[:].rearrange("p e t -> p (e t)"))
+            vv_mx.append((codes, scales))
+
+        scaled = []
+        for j in range(PACK):
+            gather_and_turn(j)
+            if j >= 2:
+                quantise_values(j - 2, scaled[j - 2])
+            if j >= 1:
+                scaled.append(scale_values(j - 1))
+        quantise_values(PACK - 2, scaled[PACK - 2])
+
+        gate_by_word = sb.tile([P, Q, PACK], F32, name="gate_by_word")
+        nc.scalar.copy(gate_by_word[:], gate[:].rearrange("p t q -> p q t"))
 
         early = mean_sq[0]
         for j in range(1, PACK - 1):
             more = sb.tile([P, PACK], F32, name="early%d" % j)
             nc.gpsimd.tensor_tensor(more[:], early[:], mean_sq[j][:], ALU.add)
             early = more
-        rms = sb.tile([P, PACK], F32, name="rms")
+        rms = big.tile([P, PACK], F32, name="rms", align_bytes=64, offset=0)
         for t in range(PACK):
             nc.scalar.activation(rms[:, t : t + 1], mean_sq[-1][:, t : t + 1], ACT.Sqrt, bias=early[:, t : t + 1])
+        factor = sb.tile([P, PACK], F32, name="factor")
+        nc.vector.tensor_tensor(factor[:], rms[:], us_t[:], ALU.mult)
 
         out_rows = out_0.rearrange("(p j) q -> p j q", j=PACK)
         out_words = out_1[0].rearrange("p c r -> p (c r)").bitcast(I32)
         o_codes = sb.tile([P, Q], U32, name="o_codes", align_bytes=64)
         o_scales = sb.tile([P, Q], U8, name="o_scales", align_bytes=64)
-        sums = []
-        for h in range(HALVES):
-            cols = slice(h * QH, (h + 1) * QH)
+
+        def form_weights(h):
             w_bf = sb.tile([P, QH, PACK], BF16, name="w_bf%d" % h, align_bytes=64)
             nc.vector.tensor_tensor(
-                w_bf[:].rearrange("p (c i) t -> p c t i", i=RUN),
-                gate_us[:, :, cols].rearrange("p t (c i) -> p c t i", i=RUN),
-                rms[:].unsqueeze(1).unsqueeze(3).to_broadcast([P, QH // RUN, PACK, RUN]),
+                w_bf[:],
+                gate_by_word[:, h * QH : (h + 1) * QH, :],
+                factor[:].unsqueeze(1).to_broadcast([P, QH, PACK]),
                 ALU.mult,
             )
+            return w_bf
+
+        def quantise_weights(h, w_bf):
             w_codes = sb.tile([P, QH], U32, name="w_codes%d" % h, align_bytes=64)
             w_scales = sb.tile([P, QH], U8, name="w_scales%d" % h, align_bytes=64)
             nc.vector.quantize_mx(w_codes[:].bitcast(FP8X4), w_scales[:], w_bf[:].rearrange("p q t -> p (q t)"))
+            return w_codes, w_scales
+
+        w_first = form_weights(0)
+        vv_last = scale_values(PACK - 1)
+        weights = [quantise_weights(0, w_first)]
+        quantise_values(PACK - 1, vv_last)
+        weights.append(quantise_weights(1, form_weights(1)))
+
+        sums = []
+        for h, (w_codes, w_scales) in enumerate(weights):
             bank = ps.tile([P, PACK, QH], F32, name="sums%d" % h, tag="products", bufs=2)
-            for j in range(PACK):
+            for j, (vv_codes, vv_scales) in enumerate(vv_mx):
                 nc.tensor.matmul_mx(
                     bank[:, j, :],
-                    lhsT=vv_codes[:, j, :].bitcast(FP8X4),
-                    lhsT_scale=vv_scales[:, j, :],
+                    lhsT=vv_codes[:].bitcast(FP8X4),
+                    lhsT_scale=vv_scales[:],
                     rhs=w_codes[:].bitcast(FP8X4),
                     rhs_scale=w_scales[:],
                     start=True,

@@ -25,6 +25,7 @@ RUN = 4
 VV_BF_BYTES = P * PACK * 2
 POOL_BYTES = T * 4
 SLOT_BYTES = I * 4
+GATE_OFFSET = PACK * POOL_BYTES - Q * PACK * 4
 
 
 def tile_attend_valuelength_pl_kernel(tc, query, keys_words, keys_scales, bias, vals, us, vsc, offs, out_0, out_1, out_2):
@@ -60,12 +61,13 @@ def tile_attend_valuelength_pl_kernel(tc, query, keys_words, keys_scales, bias, 
 
         val_rows = vals.rearrange("(p j) n -> p j n", j=PACK)
         val_pool = [big.tile([P, T], F32, name="val_pool%d" % j, align_bytes=64, offset=j * POOL_BYTES) for j in range(PACK)]
-        bias_t = load_by_slot("bias_t", bias)
         nc.sync.dma_start(val_pool[0][:], val_rows[:, 0, :])
+        bias_t = load_by_slot("bias_t", bias)
+        nc.sync.dma_start(val_pool[1][:], val_rows[:, 1, :])
         vsc_t = load_by_slot("vsc_t", vsc)
-        us_t = load_by_slot("us_t", us)
-        for j in range(1, PACK):
+        for j in range(2, PACK):
             nc.sync.dma_start(val_pool[j][:], val_rows[:, j, :])
+        us_t = load_by_slot("us_t", us)
 
         ident = sb.tile([P, P], F32, name="ident")
         make_identity(nc, ident[:])
@@ -116,7 +118,7 @@ def tile_attend_valuelength_pl_kernel(tc, query, keys_words, keys_scales, bias, 
             squares = sb.tile([P, PACK, P], BF16, name="squares%d" % j)
             part = sb.tile([P, PACK], F32, name="mean_sq%d" % j)
             for t in range(PACK):
-                for_squares = ps.tile([P, P], F32, name="for_squares", tag="for_squares", bufs=PACK)
+                for_squares = ps.tile([P, P], F32, name="for_squares", tag="quarter", bufs=PACK)
                 nc.tensor.transpose(for_squares[:], listed[:, t::PACK], ident[:])
                 nc.scalar.activation(
                     squares[:, t, :], for_squares[:], ACT.Square, scale=E**-0.5, accum_out=part[:, t : t + 1]
@@ -128,7 +130,8 @@ def tile_attend_valuelength_pl_kernel(tc, query, keys_words, keys_scales, bias, 
             turned.append(for_values)
 
         def scale_values(j):
-            vv_bf = big.tile([P, P, PACK], BF16, name="vv_bf%d" % j, align_bytes=64, offset=(j + 1) % PACK * POOL_BYTES)
+            place = (j + 1) * POOL_BYTES if j < PACK - 1 else GATE_OFFSET
+            vv_bf = big.tile([P, P, PACK], BF16, name="vv_bf%d" % j, align_bytes=64, offset=place)
             nc.vector.tensor_tensor(
                 vv_bf[:],
                 turned[j][:].rearrange("p t e -> p e t"),
@@ -152,17 +155,16 @@ def tile_attend_valuelength_pl_kernel(tc, query, keys_words, keys_scales, bias, 
                 quantise_values(j - 2, scaled[j - 2])
             if j >= 1:
                 scaled.append(scale_values(j - 1))
+        gate_by_word = big.tile([P, Q, PACK], F32, name="gate_by_word", align_bytes=64, offset=GATE_OFFSET)
+        nc.vector.tensor_copy(gate_by_word[:], gate[:].rearrange("p t q -> p q t"))
         quantise_values(PACK - 2, scaled[PACK - 2])
-
-        gate_by_word = sb.tile([P, Q, PACK], F32, name="gate_by_word")
-        nc.scalar.copy(gate_by_word[:], gate[:].rearrange("p t q -> p q t"))
 
         early = mean_sq[0]
         for j in range(1, PACK - 1):
             more = sb.tile([P, PACK], F32, name="early%d" % j)
             nc.gpsimd.tensor_tensor(more[:], early[:], mean_sq[j][:], ALU.add)
             early = more
-        rms = big.tile([P, PACK], F32, name="rms", align_bytes=64, offset=0)
+        rms = sb.tile([P, PACK], F32, name="rms")
         for t in range(PACK):
             nc.scalar.activation(rms[:, t : t + 1], mean_sq[-1][:, t : t + 1], ACT.Sqrt, bias=early[:, t : t + 1])
         factor = sb.tile([P, PACK], F32, name="factor")
@@ -189,42 +191,46 @@ def tile_attend_valuelength_pl_kernel(tc, query, keys_words, keys_scales, bias, 
             nc.vector.quantize_mx(w_codes[:].bitcast(FP8X4), w_scales[:], w_bf[:].rearrange("p q t -> p (q t)"))
             return w_codes, w_scales
 
-        w_first = form_weights(0)
+        w_bfs = [form_weights(h) for h in range(HALVES)]
+        weights = [quantise_weights(0, w_bfs[0])]
         vv_last = scale_values(PACK - 1)
-        weights = [quantise_weights(0, w_first)]
+        weights.append(quantise_weights(1, w_bfs[1]))
         quantise_values(PACK - 1, vv_last)
-        weights.append(quantise_weights(1, form_weights(1)))
 
-        sums = []
-        for h, (w_codes, w_scales) in enumerate(weights):
-            bank = ps.tile([P, PACK, QH], F32, name="sums%d" % h, tag="products", bufs=2)
-            for j, (vv_codes, vv_scales) in enumerate(vv_mx):
-                nc.tensor.matmul_mx(
-                    bank[:, j, :],
-                    lhsT=vv_codes[:].bitcast(FP8X4),
-                    lhsT_scale=vv_scales[:],
-                    rhs=w_codes[:].bitcast(FP8X4),
-                    rhs_scale=w_scales[:],
-                    start=True,
-                    stop=True,
-                )
-            sums.append(bank)
+        sums = {
+            (h, pair): ps.tile([P, 2, QH], F32, name="sums%d%d" % (h, pair), tag="quarter", bufs=PACK)
+            for pair in range(2)
+            for h in range(HALVES)
+        }
+        passes = [(h, j) for h in range(HALVES) for j in range(PACK - 1)] + [(h, PACK - 1) for h in range(HALVES)]
+        for h, j in passes:
+            nc.tensor.matmul_mx(
+                sums[h, j // 2][:, j % 2, :],
+                lhsT=vv_mx[j][0][:].bitcast(FP8X4),
+                lhsT_scale=vv_mx[j][1][:],
+                rhs=weights[h][0][:].bitcast(FP8X4),
+                rhs_scale=weights[h][1][:],
+                start=True,
+                stop=True,
+            )
 
+        o_f32 = sb.tile([P, PACK, Q], F32, name="o_f32")
+        for pair in range(2):
+            rows = slice(2 * pair, 2 * pair + 2)
+            for h in range(HALVES):
+                nc.scalar.copy(o_f32[:, rows, h * QH : (h + 1) * QH], sums[h, pair][:])
+            nc.sync.dma_start(out_rows[:, rows, :], o_f32[:, rows, :])
+        o_bf = sb.tile([P, Q, PACK], BF16, name="o_bf", align_bytes=64)
         for h in range(HALVES):
             cols = slice(h * QH, (h + 1) * QH)
-            o_bf = sb.tile([P, QH, PACK], BF16, name="o_bf%d" % h, align_bytes=64)
-            nc.scalar.copy(o_bf[:], sums[h][:].rearrange("p j q -> p q j"))
-            nc.vector.quantize_mx(o_codes[:, cols].bitcast(FP8X4), o_scales[:, cols], o_bf[:].rearrange("p q j -> p (q j)"))
-            nc.sync.dma_start(out_words[:, cols], o_codes[:, cols].bitcast(I32))
-            o_f32 = sb.tile([P, PACK, QH], F32, name="o_f32%d" % h)
-            if h < HALVES - 1:
-                nc.vector.tensor_copy(o_f32[:], sums[h][:])
-                nc.sync.dma_start(out_rows[:, :, cols], o_f32[:])
-            else:
-                nc.scalar.copy(o_f32[:], sums[h][:])
-                nc.scalar.dma_start(out_rows[:, :, cols], o_f32[:])
+            nc.vector.tensor_copy(
+                o_bf[:, cols, :].rearrange("p (c i) j -> p c j i", i=RUN),
+                o_f32[:, :, cols].rearrange("p j (c i) -> p c j i", i=RUN),
+            )
+        nc.vector.quantize_mx(o_codes[:].bitcast(FP8X4), o_scales[:], o_bf[:].rearrange("p q j -> p (q j)"))
+        nc.sync.dma_start(out_words, o_codes[:].bitcast(I32))
         for quad in range(4):
-            queue = nc.sync if quad < 2 else nc.scalar
+            queue = nc.sync if quad < 1 else nc.scalar
             queue.dma_start(
                 out_2[0, 4 * quad : 4 * quad + 4, :].bitcast(I32),
                 o_scales[32 * quad : 32 * quad + 4, :].bitcast(I32),

from contextlib import ExitStack

import concourse.mybir as mybir
from concourse.masks import make_identity

D, T, I, Q, E = 512, 2048, 512, 256, 512
FLOPS = 2 * D * I * Q + 2 * I * E * Q

F32 = mybir.dt.float32
BF16 = mybir.dt.bfloat16
I32 = mybir.dt.int32
U32 = mybir.dt.uint32
U16 = mybir.dt.uint16
U8 = mybir.dt.uint8
FP8X4 = mybir.dt.float8_e4m3fn_x4
FP4X4 = mybir.dt.float4_e2m1fn_x4
ACT = mybir.ActivationFunctionType
ALU = mybir.AluOpType

P = 128
PACK = 4
HALVES = 2
QH = Q // HALVES
RUN = 4
VV_BF_BYTES = P * PACK * 2
POOL_BYTES = T * 4
SLOT_BYTES = I * 4
GATE_OFFSET = PACK * POOL_BYTES - Q * PACK * 4


def tile_attend_valuelength_pl_kernel(tc, query, keys_words, keys_scales, bias, vals, us, vsc, offs, out_0, out_1, out_2):
    nc = tc.nc

    with ExitStack() as ctx:
        sb = ctx.enter_context(tc.tile_pool(name="sb", bufs=1))
        ring = ctx.enter_context(tc.tile_pool(name="ring", bufs=1))
        big = ctx.enter_context(tc.tile_pool(name="big", bufs=1))
        ps = ctx.enter_context(tc.psum_pool(name="ps", bufs=1))

        offsets = sb.tile([P, I // 16], U16, name="offsets")
        nc.sync.dma_start(offsets[:], offs)

        key_pool = sb.tile([P, T], U16, name="key_pool")
        nc.sync.dma_start(key_pool[:].bitcast(I32), keys_words[0].bitcast(I32))

        scale_pool = sb.tile([P, T], U8, name="scale_pool")
        nc.vector.memset(scale_pool[:].bitcast(I32), 0)
        for quad in range(4):
            nc.sync.dma_start(
                scale_pool[32 * quad : 32 * quad + 4, :].bitcast(I32),
                keys_scales[0, 4 * quad : 4 * quad + 4, :].bitcast(I32),
            )

        q_raw = sb.tile([P, PACK, Q], F32, name="q_raw")
        nc.sync.dma_start(q_raw[:], query.rearrange("(p t) q -> p t q", t=PACK))

        def load_by_slot(name, src):
            dst = sb.tile([P, PACK], F32, name=name)
            nc.sync.dma_start(dst[:], src.rearrange("(p t) o -> p (t o)", t=PACK))
            return dst

        val_rows = vals.rearrange("(p j) n -> p j n", j=PACK)
        val_pool = [big.tile([P, T], F32, name="val_pool%d" % j, align_bytes=64, offset=j * POOL_BYTES) for j in range(PACK)]
        nc.sync.dma_start(val_pool[0][:], val_rows[:, 0, :])
        bias_t = load_by_slot("bias_t", bias)
        nc.sync.dma_start(val_pool[1][:], val_rows[:, 1, :])
        vsc_t = load_by_slot("vsc_t", vsc)
        for j in range(2, PACK):
            nc.sync.dma_start(val_pool[j][:], val_rows[:, j, :])
        us_t = load_by_slot("us_t", us)

        ident = sb.tile([P, P], F32, name="ident")
        make_identity(nc, ident[:])

        key_listed = sb.tile([P, I], U16, name="key_listed")
        nc.vector.tensor_copy(key_listed[:], key_pool[:].indirect(offsets[:]))
        key_dealt = sb.tile([P, PACK, P], U16, name="key_dealt", align_bytes=64)
        nc.vector.tensor_copy(key_dealt[:], key_listed[:].rearrange("p (s t) -> p t s", t=PACK))
        scale_dealt = sb.tile([P, PACK, P], U8, name="scale_dealt", align_bytes=64)
        scale_listed = sb.tile([P, I], U8, name="scale_listed")
        nc.vector.tensor_copy(scale_listed[:], scale_pool[:].indirect(offsets[:]))
        nc.vector.tensor_copy(scale_dealt[:], scale_listed[:].rearrange("p (s t) -> p t s", t=PACK))

        q_bf = ring.tile([P, Q, PACK], BF16, name="q_bf", align_bytes=64, offset=SLOT_BYTES // 2)
        nc.scalar.copy(
            q_bf[:].rearrange("p (c i) t -> p c t i", i=RUN),
            q_raw[:].rearrange("p t (c i) -> p c t i", i=RUN),
        )
        q_codes = sb.tile([P, Q], U32, name="q_codes", align_bytes=64)
        q_scales = sb.tile([P, Q], U8, name="q_scales", align_bytes=64)
        nc.vector.quantize_mx(q_codes[:].bitcast(FP8X4), q_scales[:], q_bf[:].rearrange("p q t -> p (q t)"))

        scores = [ps.tile([P, 2, Q], F32, name="scores%d" % b, tag="products", bufs=2) for b in range(2)]
        for t in range(PACK):
            nc.tensor.matmul_mx(
                scores[t // 2][:, t % 2, :],
                lhsT=key_dealt[:, t, :].bitcast(FP4X4),
                lhsT_scale=scale_dealt[:, t, :],
                rhs=q_codes[:].bitcast(FP8X4),
                rhs_scale=q_scales[:],
                start=True,
                stop=True,
            )
        gate = sb.tile([P, PACK, Q], F32, name="gate")
        for t in range(PACK):
            nc.scalar.activation(gate[:, t, :], scores[t // 2][:, t % 2, :], ACT.Sigmoid, bias=bias_t[:, t : t + 1])

        root_table = sb.tile([P, 1], F32, name="root_table")
        nc.scalar.activation(root_table[:], gate[:, PACK - 1, 0:1], ACT.Sqrt)

        vv_mx = []
        mean_sq = []
        turned = []

        def gather_and_turn(j):
            listed = ring.tile([P, I], F32, name="val_listed%d" % j, align_bytes=64, offset=(j % 2) * SLOT_BYTES)
            nc.vector.tensor_copy(listed[:], val_pool[j][:].indirect(offsets[:]))
            squares = sb.tile([P, PACK, P], BF16, name="squares%d" % j)
            part = sb.tile([P, PACK], F32, name="mean_sq%d" % j)
            for t in range(PACK):
                for_squares = ps.tile([P, P], F32, name="for_squares", tag="quarter", bufs=PACK)
                nc.tensor.transpose(for_squares[:], listed[:, t::PACK], ident[:])
                nc.scalar.activation(
                    squares[:, t, :], for_squares[:], ACT.Square, scale=E**-0.5, accum_out=part[:, t : t + 1]
                )
            for_values = ps.tile([P, PACK, P], F32, name="for_values", tag="for_values", bufs=2)
            for t in range(PACK):
                nc.tensor.transpose(for_values[:, t, :], listed[:, t::PACK], ident[:])
            mean_sq.append(part)
            turned.append(for_values)

        def scale_values(j):
            place = (j + 1) * POOL_BYTES if j < PACK - 1 else GATE_OFFSET
            vv_bf = big.tile([P, P, PACK], BF16, name="vv_bf%d" % j, align_bytes=64, offset=place)
            nc.vector.tensor_tensor(
                vv_bf[:],
                turned[j][:].rearrange("p t e -> p e t"),
                vsc_t[:].unsqueeze(1).to_broadcast([P, P, PACK]),
                ALU.mult,
            )
            return vv_bf

        def quantise_values(j, vv_bf):
            codes = big.tile(
                [P, P], U32, name="vv_codes%d" % j, align_bytes=64, offset=(j + 2) % PACK * POOL_BYTES + VV_BF_BYTES
            )
            scales = sb.tile([P, P], U8, name="vv_scales%d" % j, align_bytes=64)
            nc.vector.quantize_mx(codes[:].bitcast(FP8X4), scales[:], vv_bf[:].rearrange("p e t -> p (e t)"))
            vv_mx.append((codes, scales))

        scaled = []
        for j in range(PACK):
            gather_and_turn(j)
            if j >= 2:
                quantise_values(j - 2, scaled[j - 2])
            if j >= 1:
                scaled.append(scale_values(j - 1))
        gate_by_word = big.tile([P, Q, PACK], F32, name="gate_by_word", align_bytes=64, offset=GATE_OFFSET)
        nc.vector.tensor_copy(gate_by_word[:], gate[:].rearrange("p t q -> p q t"))
        quantise_values(PACK - 2, scaled[PACK - 2])

        early = mean_sq[0]
        for j in range(1, PACK - 1):
            more = sb.tile([P, PACK], F32, name="early%d" % j)
            nc.gpsimd.tensor_tensor(more[:], early[:], mean_sq[j][:], ALU.add)
            early = more
        rms = sb.tile([P, PACK], F32, name="rms")
        for t in range(PACK):
            nc.scalar.activation(rms[:, t : t + 1], mean_sq[-1][:, t : t + 1], ACT.Sqrt, bias=early[:, t : t + 1])
        factor = sb.tile([P, PACK], F32, name="factor")
        nc.vector.tensor_tensor(factor[:], rms[:], us_t[:], ALU.mult)

        out_rows = out_0.rearrange("(p j) q -> p j q", j=PACK)
        out_words = out_1[0].rearrange("p c r -> p (c r)").bitcast(I32)
        o_codes = sb.tile([P, Q], U32, name="o_codes", align_bytes=64)
        o_scales = sb.tile([P, Q], U8, name="o_scales", align_bytes=64)

        def form_weights(h):
            w_bf = sb.tile([P, QH, PACK], BF16, name="w_bf%d" % h, align_bytes=64)
            nc.vector.tensor_tensor(
                w_bf[:],
                gate_by_word[:, h * QH : (h + 1) * QH, :],
                factor[:].unsqueeze(1).to_broadcast([P, QH, PACK]),
                ALU.mult,
            )
            return w_bf

        def quantise_weights(h, w_bf):
            w_codes = sb.tile([P, QH], U32, name="w_codes%d" % h, align_bytes=64)
            w_scales = sb.tile([P, QH], U8, name="w_scales%d" % h, align_bytes=64)
            nc.vector.quantize_mx(w_codes[:].bitcast(FP8X4), w_scales[:], w_bf[:].rearrange("p q t -> p (q t)"))
            return w_codes, w_scales

        w_bfs = [form_weights(h) for h in range(HALVES)]
        weights = [quantise_weights(0, w_bfs[0])]
        vv_last = scale_values(PACK - 1)
        weights.append(quantise_weights(1, w_bfs[1]))
        quantise_values(PACK - 1, vv_last)

        sums = {
            (h, pair): ps.tile([P, 2, QH], F32, name="sums%d%d" % (h, pair), tag="quarter", bufs=PACK)
            for pair in range(2)
            for h in range(HALVES)
        }
        passes = [(h, j) for h in range(HALVES) for j in range(PACK - 1)] + [(h, PACK - 1) for h in range(HALVES)]
        for h, j in passes:
            nc.tensor.matmul_mx(
                sums[h, j // 2][:, j % 2, :],
                lhsT=vv_mx[j][0][:].bitcast(FP8X4),
                lhsT_scale=vv_mx[j][1][:],
                rhs=weights[h][0][:].bitcast(FP8X4),
                rhs_scale=weights[h][1][:],
                start=True,
                stop=True,
            )

        o_f32 = sb.tile([P, PACK, Q], F32, name="o_f32")
        for pair in range(2):
            rows = slice(2 * pair, 2 * pair + 2)
            for h in range(HALVES):
                nc.scalar.copy(o_f32[:, rows, h * QH : (h + 1) * QH], sums[h, pair][:])
            nc.sync.dma_start(out_rows[:, rows, :], o_f32[:, rows, :])
        o_bf = sb.tile([P, Q, PACK], BF16, name="o_bf", align_bytes=64)
        for h in range(HALVES):
            cols = slice(h * QH, (h + 1) * QH)
            nc.vector.tensor_copy(
                o_bf[:, cols, :].rearrange("p (c i) j -> p c j i", i=RUN),
                o_f32[:, :, cols].rearrange("p j (c i) -> p c j i", i=RUN),
            )
        nc.vector.quantize_mx(o_codes[:].bitcast(FP8X4), o_scales[:], o_bf[:].rearrange("p q j -> p (q j)"))
        nc.sync.dma_start(out_words, o_codes[:].bitcast(I32))
        for quad in range(4):
            queue = nc.sync if quad < 1 else nc.scalar
            queue.dma_start(
                out_2[0, 4 * quad : 4 * quad + 4, :].bitcast(I32),
                o_scales[32 * quad : 32 * quad + 4, :].bitcast(I32),
            )
